import numpy as np
import ml_dtypes


def mxq(x, axis, fmt="e4m3"):
    dtype, down = {"e4m3": (ml_dtypes.float8_e4m3fn, 7), "e5m2": (ml_dtypes.float8_e5m2, 14)}[fmt]
    v = np.moveaxis(np.asarray(x, np.float32).astype(ml_dtypes.bfloat16).astype(np.float64), axis, -1)
    blocks = v.reshape(v.shape[:-1] + (-1, 32))
    amax = np.abs(blocks).max(-1, keepdims=True)
    byte = np.maximum(np.where(amax > 0, np.frexp(amax)[1] - 1 + 127, 0) - down, 1)
    scale = np.exp2(byte - 127.0)
    codes = (blocks / scale).astype(np.float32).astype(dtype).astype(np.float64)
    return np.moveaxis((codes * scale).reshape(v.shape), -1, axis)


WIDE = False


def mx_kscale(k):
    if not WIDE:
        return np.ones(k)
    levels = np.array([10, -10, 5, -5, 0])
    if k % 512:
        return np.exp2(np.random.permutation(np.resize(levels, k // 32))).repeat(32)
    a = np.empty((k // 512, 16))
    for p in range(k // 512):
        a[p, :8] = np.random.permutation(np.resize(levels, 8))
        for g in range(8):
            far = levels[np.abs(levels - a[p, g]) >= 10]
            a[p, g + 8] = far[np.random.randint(len(far))]
    return np.exp2(a.ravel()).repeat(32)


def f64(x):
    return np.asarray(x).astype(np.float64)


def striped(idx):
    return np.tile(idx.reshape(-1, 16).T, (8, 1)).astype(np.uint16)


def unstriped(offs):
    return offs[:16].T.reshape(-1).astype(np.int64)


def striped8(idx):
    return np.concatenate([x.reshape(-1, 16).T for x in idx]).astype(np.uint16)


def runs(offs, k):
    lists = np.stack([offs[16 * r : 16 * r + 16].T.reshape(-1) for r in range(8)]).astype(np.int64)
    return lists[np.arange(k) % 512 // 64]


def pack_weight(w):
    k, n = w.shape
    w = f64(np.asarray(w, np.float32).astype(ml_dtypes.bfloat16)).reshape(k // 32, 32, n)
    amax = np.abs(w).max(1)
    byte = np.clip(np.where(amax > 0, np.frexp(amax)[1] - 1 + 127 - 7, 1), 1, 254)
    scaled = (w * np.exp2(127.0 - byte)[:, None, :]).reshape(k, n).astype(np.float32)
    words = np.ascontiguousarray(scaled.reshape(k // 512, 128, 4, n).transpose(0, 1, 3, 2)).astype(ml_dtypes.float8_e4m3fn).view(np.uint8)
    return words, np.ascontiguousarray(byte.astype(np.uint8).reshape(k // 512, 16, n))


def unpack_weight(words, scales):
    g, p, n, _ = words.shape
    vals = np.ascontiguousarray(words).view(ml_dtypes.float8_e4m3fn).astype(np.float64) * np.repeat(np.exp2(scales.astype(np.float64) - 127.0), 8, axis=1)[..., None]
    return vals.transpose(0, 1, 3, 2).reshape(g * 512, n)

def planes(y):
    n, m = y.shape
    v = y.astype(np.float32).astype(ml_dtypes.bfloat16).astype(np.float64).reshape(n // 32, 32, m)
    top = np.abs(v).max(1)
    byte = np.clip(np.where(top > 0, np.frexp(top)[1] - 1 + 127 - 7, 1), 1, 254)
    codes = (v * np.exp2(127.0 - byte)[:, None, :]).reshape(n, m).astype(np.float32).astype(ml_dtypes.float8_e4m3fn).view(np.uint8)
    words = codes.reshape(n // 512, 128, 4, m).transpose(0, 1, 3, 2)
    return np.ascontiguousarray(words), np.ascontiguousarray(byte.astype(np.uint8).reshape(n // 512, 16, m))


K, T, S, V, H, C = 512, 2048, 512, 256, 512, 512


def setup_inputs():
    n = np.random.standard_normal
    s = mx_kscale(K)[:, None]
    packed_xT = pack_weight(n((K, T)) * s)
    packed_w1 = pack_weight(n((K, H)) / np.sqrt(K) / s)
    return {
        "x_words": packed_xT[0],
        "x_scales": packed_xT[1],
        "w1_words": packed_w1[0],
        "w1_scales": packed_w1[1],
        "gs": (np.random.uniform(0.5, 1.5, (K, 1)) / s).astype(np.float32),
        "offs": striped(np.random.permutation(T)[:S]),
        "c1": striped8(np.stack([np.random.permutation(S)[:V] for _ in range(8)])),
        "c2": striped8(np.stack([np.random.permutation(S)[:V] for _ in range(8)])),
        "cand": striped(np.random.permutation(T)[:C]),
    }


def reference(x_words, x_scales, w1_words, w1_scales, gs, offs, c1, c2, cand):
    x_cand = unpack_weight(x_words, x_scales)[:, unstriped(cand)]
    xq = unpack_weight(x_words, x_scales)[:, unstriped(offs)]
    th = np.tanh(0.5 * ((unpack_weight(w1_words, w1_scales).T @ xq)))
    p = (th[np.arange(H)[:, None], runs(c1, H)]) * (th[np.arange(H)[:, None], runs(c2, H)])
    z = f64(gs) * (np.log((p + 1.125) / (-1.0 * p + 1.125)))
    out_0 = 0.0625 * ((x_cand.T @ mxq(z, 0, "e4m3")))
    return (out_0,) + planes(out_0)

@@ -1,0 +1,151 @@
+from contextlib import ExitStack
+
+import concourse.mybir as mybir
+
+K, T, S, V, H, C = 512, 2048, 512, 256, 512, 512
+FLOPS = 2 * K * H * S + 2 * K * C * V
+
+F32 = mybir.dt.float32
+BF16 = mybir.dt.bfloat16
+I32 = mybir.dt.int32
+U32 = mybir.dt.uint32
+U16 = mybir.dt.uint16
+U8 = mybir.dt.uint8
+FP8X4 = mybir.dt.float8_e4m3fn_x4
+ACT = mybir.ActivationFunctionType
+ALU = mybir.AluOpType
+
+P = 128
+PACK = 4
+HALVES = 2
+VH = V // HALVES
+
+
+def load_scale_rows(queue, plane, rows):
+    for q in range(4):
+        queue.dma_start(out=plane[32 * q : 32 * q + 4, :].bitcast(I32), in_=rows[4 * q : 4 * q + 4, :].bitcast(I32))
+
+
+def tile_picked_chkmsg_none_po_kernel(
+    tc, x_words, x_scales, w1_words, w1_scales, gs, offs, c1, c2, cand, out_0, out_1, out_2
+):
+    nc = tc.nc
+    with ExitStack() as ctx:
+        keep = ctx.enter_context(tc.tile_pool(name="keep", bufs=1))
+        psum = ctx.enter_context(tc.psum_pool(name="psum", bufs=1))
+
+        offs_t = keep.tile([P, S // 16], U16, name="offs_t")
+        cand_t = keep.tile([P, C // 16], U16, name="cand_t")
+        c1_t = keep.tile([P, V // 16], U16, name="c1_t")
+        c2_t = keep.tile([P, V // 16], U16, name="c2_t")
+        xs = keep.tile([P, T], U8, name="xs", align_bytes=64)
+        ww = keep.tile([P, H], U32, name="ww", align_bytes=64)
+        ws = keep.tile([P, H], U8, name="ws", align_bytes=64)
+        gain = keep.tile([P, PACK], F32, name="gain")
+        offset = keep.tile([P, 1], F32, name="offset")
+        warm = keep.tile([P, 1], F32, name="warm", tag="table", align_bytes=64)
+        warm2 = keep.tile([P, 1], F32, name="warm2")
+
+        nc.gpsimd.memset(xs[:, : T // 2].bitcast(I32), 0)
+        nc.vector.memset(xs[:, T // 2 :].bitcast(I32), 0)
+        nc.vector.memset(offset[:], 1.125)
+        nc.vector.memset(ws[:].bitcast(I32), 0)
+        nc.scalar.activation(out=warm[:], in_=offset[:], func=ACT.Tanh)
+        xw = keep.tile([P, T], U32, name="xw", tag="table", align_bytes=64)
+
+        nc.gpsimd.dma_start(out=ww[:].bitcast(I32), in_=w1_words[0].rearrange("p n t -> p (n t)").bitcast(I32))
+        nc.sync.dma_start(offs_t[:], offs)
+        nc.sync.dma_start(cand_t[:], cand)
+        nc.sync.dma_start(c1_t[:], c1)
+        nc.sync.dma_start(c2_t[:], c2)
+        load_scale_rows(nc.sync, xs, x_scales[0])
+        load_scale_rows(nc.sync, ws, w1_scales[0])
+        nc.sync.dma_start(out=xw[:].bitcast(I32), in_=x_words[0].rearrange("p n t -> p (n t)").bitcast(I32))
+        nc.gpsimd.dma_start(out=gain[:], in_=gs.rearrange("(p t) o -> p (t o)", t=PACK))
+
+        xq_s = keep.tile([P, S], U8, name="xq_s", align_bytes=64)
+        xq_w = keep.tile([P, S], U32, name="xq_w", align_bytes=64)
+        wd_w = keep.tile([P, H], U32, name="wd_w", align_bytes=64)
+        wd_s = keep.tile([P, H], U8, name="wd_s", align_bytes=64)
+        xc_raw = keep.tile([P, C], U8, name="xc_raw", align_bytes=64)
+        xc_s = keep.tile([P, C], U8, name="xc_s", align_bytes=64)
+        xc_w = keep.tile([P, C], U32, name="xc_w", align_bytes=64)
+
+        nc.vector.tensor_copy(xq_s[:], xs[:].indirect(offs_t[:]))
+        nc.vector.tensor_copy(
+            out=wd_w[:].bitcast(I32).rearrange("p (t m) -> p m t", t=PACK),
+            in_=ww[:].bitcast(I32).rearrange("p (m t) -> p m t", t=PACK),
+        )
+        nc.vector.tensor_copy(
+            out=wd_s[:].rearrange("p (t m) -> p t m", t=PACK), in_=ws[:].rearrange("p (m t) -> p t m", t=PACK)
+        )
+        nc.vector.tensor_copy(xq_w[:], xw[:].indirect(offs_t[:]))
+
+        th = []
+        for t in range(PACK):
+            acc = psum.tile([P, S], F32, name="acc%d" % t)
+            cols = slice(P * t, P * (t + 1))
+            nc.tensor.matmul_mx(
+                out=acc[:], lhsT=wd_w[:, cols].bitcast(FP8X4), lhsT_scale=wd_s[:, cols],
+                rhs=xq_w[:].bitcast(FP8X4), rhs_scale=xq_s[:], start=True, stop=True,
+            )
+            row = keep.tile([P, S], F32, name="th%d" % t, align_bytes=64)
+            nc.scalar.activation(out=row[:], in_=acc[:], func=ACT.Tanh, scale=0.5)
+            th.append(row)
+        nc.scalar.activation(out=warm2[:], in_=th[PACK - 1][:, 0:1], func=ACT.Ln, bias=offset[:])
+
+        nc.vector.tensor_copy(xc_raw[:], xs[:].indirect(cand_t[:]))
+        nc.vector.tensor_copy(xc_w[:].rearrange("p (t m) -> p m t", t=PACK), xw[:].indirect(cand_t[:]))
+        nc.vector.tensor_copy(
+            out=xc_s[:].rearrange("p (t m) -> p t m", t=PACK), in_=xc_raw[:].rearrange("p (m t) -> p t m", t=PACK)
+        )
+
+        o_w = keep.tile([P, V], U32, name="o_w", align_bytes=64)
+        o_s = keep.tile([P, V], U8, name="o_s", align_bytes=64)
+        out_rows = out_0.rearrange("(p t) v -> p t v", t=PACK)
+        ups, downs = [], []
+        for h in range(HALVES):
+            entries = slice(h * VH // 16, (h + 1) * VH // 16)
+            first = keep.tile([P, PACK, VH], F32, name="first%d" % h, tag="first", align_bytes=64)
+            prod = keep.tile([P, PACK, VH], F32, name="prod%d" % h, align_bytes=64)
+            for t in range(PACK):
+                nc.vector.tensor_copy(first[:, t, :], th[t][:].indirect(c1_t[:, entries]))
+                if t > 0:
+                    nc.vector.tensor_tensor(prod[:, t - 1, :], th[t - 1][:].indirect(c2_t[:, entries]), first[:, t - 1, :], ALU.mult)
+            nc.vector.tensor_tensor(prod[:, PACK - 1, :], th[PACK - 1][:].indirect(c2_t[:, entries]), first[:, PACK - 1, :], ALU.mult)
+            up = keep.tile([P, VH, PACK], F32, name="up%d" % h, align_bytes=64)
+            down = keep.tile([P, VH, PACK], F32, name="down%d" % h, align_bytes=64)
+            src = prod[:].rearrange("p t (c i) -> p c t i", i=4)
+            nc.scalar.activation(out=up[:].rearrange("p (c i) t -> p c t i", i=4), in_=src, func=ACT.Ln, bias=offset[:], scale=1.0)
+            nc.scalar.activation(out=down[:].rearrange("p (c i) t -> p c t i", i=4), in_=src, func=ACT.Ln, bias=offset[:], scale=-1.0)
+            ups.append(up)
+            downs.append(down)
+
+        for h in range(HALVES):
+            cols = slice(h * VH, (h + 1) * VH)
+            diff = keep.tile([P, VH, PACK], F32, name="diff%d" % h, align_bytes=64)
+            nc.vector.tensor_tensor(diff[:], ups[h][:], downs[h][:], ALU.subtract)
+            z = keep.tile([P, VH, PACK], BF16, name="z%d" % h, align_bytes=64)
+            nc.vector.tensor_tensor(z[:], diff[:], gain[:].unsqueeze(1).to_broadcast([P, VH, PACK]), ALU.mult)
+            z_w = keep.tile([P, VH], U32, name="z_w%d" % h, align_bytes=64)
+            z_s = keep.tile([P, VH], U8, name="z_s%d" % h, align_bytes=64)
+            nc.vector.quantize_mx(out=z_w[:].bitcast(FP8X4), scales=z_s[:], in_=z[:].rearrange("p v t -> p (v t)"))
+            score = psum.tile([P, PACK, VH], F32, name="score%d" % h)
+            for t in range(PACK):
+                rows = slice(P * t, P * (t + 1))
+                nc.tensor.matmul_mx(
+                    out=score[:, t, :], lhsT=xc_w[:, rows].bitcast(FP8X4), lhsT_scale=xc_s[:, rows],
+                    rhs=z_w[:].bitcast(FP8X4), rhs_scale=z_s[:], start=True, stop=True,
+                )
+            y16 = keep.tile([P, VH, PACK], BF16, name="y16_%d" % h, align_bytes=64)
+            nc.scalar.activation(out=y16[:], in_=score[:].rearrange("p t v -> p v t"), func=ACT.Copy, scale=0.0625)
+            y = keep.tile([P, PACK, VH], F32, name="y%d" % h, align_bytes=64)
+            nc.scalar.activation(out=y[:], in_=score[:], func=ACT.Copy, scale=0.0625)
+            nc.sync.dma_start(out=out_rows[:, :, cols], in_=y[:])
+            nc.vector.quantize_mx(
+                out=o_w[:, cols].bitcast(FP8X4), scales=o_s[:, cols], in_=y16[:].rearrange("p v t -> p (v t)")
+            )
+            nc.sync.dma_start(out=out_1[0].rearrange("p n t -> p (n t)").bitcast(I32)[:, cols], in_=o_w[:, cols].bitcast(I32))
+        for q in range(4):
+            queue = nc.sync if q % 2 else nc.scalar
+            queue.dma_start(out=out_2[0, 4 * q : 4 * q + 4, :].bitcast(I32), in_=o_s[32 * q : 32 * q + 4, :].bitcast(I32))

@@ -40,28 +40,31 @@ def tile_picked_chkmsg_none_po_kernel(
         c2_t = keep.tile([P, V // 16], U16, name="c2_t")
         xs = keep.tile([P, T], U8, name="xs", align_bytes=64)
         ww = keep.tile([P, H], U32, name="ww", align_bytes=64)
-        ws = keep.tile([P, H], U8, name="ws", align_bytes=64)
+        ws = keep.tile([P, H], U8, name="ws", tag="ws", align_bytes=64)
         gain = keep.tile([P, PACK], F32, name="gain")
         offset = keep.tile([P, 1], F32, name="offset")
-        warm = keep.tile([P, 1], F32, name="warm", tag="table", align_bytes=64)
+        warm = keep.tile([P, 1], F32, name="warm")
         warm2 = keep.tile([P, 1], F32, name="warm2")
 
-        nc.gpsimd.memset(xs[:, : T // 2].bitcast(I32), 0)
-        nc.vector.memset(xs[:, T // 2 :].bitcast(I32), 0)
-        nc.vector.memset(offset[:], 1.125)
-        nc.vector.memset(ws[:].bitcast(I32), 0)
-        nc.scalar.activation(out=warm[:], in_=offset[:], func=ACT.Tanh)
-        xw = keep.tile([P, T], U32, name="xw", tag="table", align_bytes=64)
+        nc.gpsimd.memset(offset[:], 1.125)
+        nc.gpsimd.memset(ws[:].bitcast(I32), 0)
+        xw = keep.tile([P, T], U32, name="xw", align_bytes=64)
 
-        nc.gpsimd.dma_start(out=ww[:].bitcast(I32), in_=w1_words[0].rearrange("p n t -> p (n t)").bitcast(I32))
         nc.sync.dma_start(offs_t[:], offs)
+        for q in range(4):
+            queue = nc.sync if q == 3 else nc.scalar
+            queue.dma_start(
+                out=xs[32 * q : 32 * q + 32, :].bitcast(I32),
+                in_=x_scales[0, 4 * q : 4 * q + 4, :].bitcast(I32).unsqueeze(0).to_broadcast([8, 4, T // 4]),
+            )
         nc.sync.dma_start(cand_t[:], cand)
+        nc.sync.dma_start(out=xw[:].bitcast(I32), in_=x_words[0].rearrange("p n t -> p (n t)").bitcast(I32))
+        nc.sync.dma_start(out=ww[:].bitcast(I32), in_=w1_words[0].rearrange("p n t -> p (n t)").bitcast(I32))
+        nc.scalar.activation(out=warm[:], in_=offset[:], func=ACT.Tanh)
+        load_scale_rows(nc.sync, ws, w1_scales[0])
         nc.sync.dma_start(c1_t[:], c1)
         nc.sync.dma_start(c2_t[:], c2)
-        load_scale_rows(nc.sync, xs, x_scales[0])
-        load_scale_rows(nc.sync, ws, w1_scales[0])
-        nc.sync.dma_start(out=xw[:].bitcast(I32), in_=x_words[0].rearrange("p n t -> p (n t)").bitcast(I32))
-        nc.gpsimd.dma_start(out=gain[:], in_=gs.rearrange("(p t) o -> p (t o)", t=PACK))
+        nc.sync.dma_start(out=gain[:], in_=gs.rearrange("(p t) o -> p (t o)", t=PACK))
 
         xq_s = keep.tile([P, S], U8, name="xq_s", align_bytes=64)
         xq_w = keep.tile([P, S], U32, name="xq_w", align_bytes=64)
@@ -69,9 +72,13 @@ def tile_picked_chkmsg_none_po_kernel(
         wd_s = keep.tile([P, H], U8, name="wd_s", align_bytes=64)
         xc_raw = keep.tile([P, C], U8, name="xc_raw", align_bytes=64)
         xc_s = keep.tile([P, C], U8, name="xc_s", align_bytes=64)
-        xc_w = keep.tile([P, C], U32, name="xc_w", align_bytes=64)
 
         nc.vector.tensor_copy(xq_s[:], xs[:].indirect(offs_t[:]))
+        nc.vector.tensor_copy(xc_raw[:], xs[:].indirect(cand_t[:]))
+        nc.vector.tensor_copy(
+            out=xc_s[:].rearrange("p (t m) -> p t m", t=PACK), in_=xc_raw[:].rearrange("p (m t) -> p t m", t=PACK)
+        )
+        nc.vector.tensor_copy(xq_w[:], xw[:].indirect(offs_t[:]))
         nc.vector.tensor_copy(
             out=wd_w[:].bitcast(I32).rearrange("p (t m) -> p m t", t=PACK),
             in_=ww[:].bitcast(I32).rearrange("p (m t) -> p m t", t=PACK),
@@ -79,7 +86,6 @@ def tile_picked_chkmsg_none_po_kernel(
         nc.vector.tensor_copy(
             out=wd_s[:].rearrange("p (t m) -> p t m", t=PACK), in_=ws[:].rearrange("p (m t) -> p t m", t=PACK)
         )
-        nc.vector.tensor_copy(xq_w[:], xw[:].indirect(offs_t[:]))
 
         th = []
         for t in range(PACK):
@@ -94,25 +100,25 @@ def tile_picked_chkmsg_none_po_kernel(
             th.append(row)
         nc.scalar.activation(out=warm2[:], in_=th[PACK - 1][:, 0:1], func=ACT.Ln, bias=offset[:])
 
-        nc.vector.tensor_copy(xc_raw[:], xs[:].indirect(cand_t[:]))
+        xc_w = keep.tile([P, C], U32, name="xc_w", tag="ws", align_bytes=64)
         nc.vector.tensor_copy(xc_w[:].rearrange("p (t m) -> p m t", t=PACK), xw[:].indirect(cand_t[:]))
-        nc.vector.tensor_copy(
-            out=xc_s[:].rearrange("p (t m) -> p t m", t=PACK), in_=xc_raw[:].rearrange("p (m t) -> p t m", t=PACK)
-        )
 
         o_w = keep.tile([P, V], U32, name="o_w", align_bytes=64)
         o_s = keep.tile([P, V], U8, name="o_s", align_bytes=64)
         out_rows = out_0.rearrange("(p t) v -> p t v", t=PACK)
+        first = keep.tile([P, PACK, V], F32, name="first", align_bytes=64)
+        second = keep.tile([P, PACK, VH], F32, name="second", tag="second", align_bytes=64)
+        for t in range(PACK):
+            nc.vector.tensor_copy(first[:, t, :], th[t][:].indirect(c1_t[:]))
+            nc.vector.tensor_copy(second[:, t, :], th[t][:].indirect(c2_t[:, : VH // 16]))
+        prod_a = keep.tile([P, PACK, VH], F32, name="prod_a", align_bytes=64)
+        nc.vector.tensor_tensor(prod_a[:], first[:, :, :VH], second[:], ALU.mult)
+        prod_b = keep.tile([P, PACK, VH], F32, name="prod_b", tag="second", align_bytes=64)
+        for t in range(PACK):
+            nc.vector.tensor_tensor(prod_b[:, t, :], th[t][:].indirect(c2_t[:, VH // 16 :]), first[:, t, VH:], ALU.mult)
+
         ups, downs = [], []
-        for h in range(HALVES):
-            entries = slice(h * VH // 16, (h + 1) * VH // 16)
-            first = keep.tile([P, PACK, VH], F32, name="first%d" % h, tag="first", align_bytes=64)
-            prod = keep.tile([P, PACK, VH], F32, name="prod%d" % h, align_bytes=64)
-            for t in range(PACK):
-                nc.vector.tensor_copy(first[:, t, :], th[t][:].indirect(c1_t[:, entries]))
-                if t > 0:
-                    nc.vector.tensor_tensor(prod[:, t - 1, :], th[t - 1][:].indirect(c2_t[:, entries]), first[:, t - 1, :], ALU.mult)
-            nc.vector.tensor_tensor(prod[:, PACK - 1, :], th[PACK - 1][:].indirect(c2_t[:, entries]), first[:, PACK - 1, :], ALU.mult)
+        for h, prod in enumerate((prod_a, prod_b)):
             up = keep.tile([P, VH, PACK], F32, name="up%d" % h, align_bytes=64)
             down = keep.tile([P, VH, PACK], F32, name="down%d" % h, align_bytes=64)
             src = prod[:].rearrange("p t (c i) -> p c t i", i=4)
@@ -130,18 +136,21 @@ def tile_picked_chkmsg_none_po_kernel(
             z_w = keep.tile([P, VH], U32, name="z_w%d" % h, align_bytes=64)
             z_s = keep.tile([P, VH], U8, name="z_s%d" % h, align_bytes=64)
             nc.vector.quantize_mx(out=z_w[:].bitcast(FP8X4), scales=z_s[:], in_=z[:].rearrange("p v t -> p (v t)"))
-            score = psum.tile([P, PACK, VH], F32, name="score%d" % h)
-            for t in range(PACK):
-                rows = slice(P * t, P * (t + 1))
-                nc.tensor.matmul_mx(
-                    out=score[:, t, :], lhsT=xc_w[:, rows].bitcast(FP8X4), lhsT_scale=xc_s[:, rows],
-                    rhs=z_w[:].bitcast(FP8X4), rhs_scale=z_s[:], start=True, stop=True,
-                )
-            y16 = keep.tile([P, VH, PACK], BF16, name="y16_%d" % h, align_bytes=64)
-            nc.scalar.activation(out=y16[:], in_=score[:].rearrange("p t v -> p v t"), func=ACT.Copy, scale=0.0625)
             y = keep.tile([P, PACK, VH], F32, name="y%d" % h, align_bytes=64)
-            nc.scalar.activation(out=y[:], in_=score[:], func=ACT.Copy, scale=0.0625)
+            for pair in range(2):
+                score = psum.tile([P, 2, VH], F32, name="score%d_%d" % (h, pair))
+                for j in range(2):
+                    rows = slice(P * (2 * pair + j), P * (2 * pair + j + 1))
+                    nc.tensor.matmul_mx(
+                        out=score[:, j, :], lhsT=xc_w[:, rows].bitcast(FP8X4), lhsT_scale=xc_s[:, rows],
+                        rhs=z_w[:].bitcast(FP8X4), rhs_scale=z_s[:], start=True, stop=True,
+                    )
+                nc.scalar.activation(out=y[:, 2 * pair : 2 * pair + 2, :], in_=score[:], func=ACT.Copy, scale=0.0625)
             nc.sync.dma_start(out=out_rows[:, :, cols], in_=y[:])
+            y16 = keep.tile([P, VH, PACK], BF16, name="y16_%d" % h, align_bytes=64)
+            nc.vector.tensor_copy(
+                out=y16[:].rearrange("p (c i) t -> p c t i", i=4), in_=y[:].rearrange("p t (c i) -> p c t i", i=4)
+            )
             nc.vector.quantize_mx(
                 out=o_w[:, cols].bitcast(FP8X4), scales=o_s[:, cols], in_=y16[:].rearrange("p v t -> p (v t)")
             )

@@ -46,21 +46,19 @@ def tile_picked_chkmsg_none_po_kernel(
         warm = keep.tile([P, 1], F32, name="warm")
         warm2 = keep.tile([P, 1], F32, name="warm2")
 
-        nc.gpsimd.memset(offset[:], 1.125)
-        nc.gpsimd.memset(ws[:].bitcast(I32), 0)
+        nc.gpsimd.memset(xs[:].bitcast(I32), 0)
+        nc.vector.memset(offset[:], 1.125)
+        nc.vector.memset(ws[:].bitcast(I32), 0)
+        nc.scalar.activation(out=warm[:], in_=offset[:], func=ACT.Tanh)
         xw = keep.tile([P, T], U32, name="xw", align_bytes=64)
+        x_rows = x_words[0].rearrange("p n t -> p (n t)").bitcast(I32)
 
         nc.sync.dma_start(offs_t[:], offs)
-        for q in range(4):
-            queue = nc.sync if q == 3 else nc.scalar
-            queue.dma_start(
-                out=xs[32 * q : 32 * q + 32, :].bitcast(I32),
-                in_=x_scales[0, 4 * q : 4 * q + 4, :].bitcast(I32).unsqueeze(0).to_broadcast([8, 4, T // 4]),
-            )
+        nc.sync.dma_start(out=xw[:, : T // 2].bitcast(I32), in_=x_rows[:, : T // 2])
+        load_scale_rows(nc.sync, xs, x_scales[0])
         nc.sync.dma_start(cand_t[:], cand)
-        nc.sync.dma_start(out=xw[:].bitcast(I32), in_=x_words[0].rearrange("p n t -> p (n t)").bitcast(I32))
+        nc.sync.dma_start(out=xw[:, T // 2 :].bitcast(I32), in_=x_rows[:, T // 2 :])
         nc.sync.dma_start(out=ww[:].bitcast(I32), in_=w1_words[0].rearrange("p n t -> p (n t)").bitcast(I32))
-        nc.scalar.activation(out=warm[:], in_=offset[:], func=ACT.Tanh)
         load_scale_rows(nc.sync, ws, w1_scales[0])
         nc.sync.dma_start(c1_t[:], c1)
         nc.sync.dma_start(c2_t[:], c2)
@@ -74,10 +72,6 @@ def tile_picked_chkmsg_none_po_kernel(
         xc_s = keep.tile([P, C], U8, name="xc_s", align_bytes=64)
 
         nc.vector.tensor_copy(xq_s[:], xs[:].indirect(offs_t[:]))
-        nc.vector.tensor_copy(xc_raw[:], xs[:].indirect(cand_t[:]))
-        nc.vector.tensor_copy(
-            out=xc_s[:].rearrange("p (t m) -> p t m", t=PACK), in_=xc_raw[:].rearrange("p (m t) -> p t m", t=PACK)
-        )
         nc.vector.tensor_copy(xq_w[:], xw[:].indirect(offs_t[:]))
         nc.vector.tensor_copy(
             out=wd_w[:].bitcast(I32).rearrange("p (t m) -> p m t", t=PACK),
@@ -85,6 +79,10 @@ def tile_picked_chkmsg_none_po_kernel(
         )
         nc.vector.tensor_copy(
             out=wd_s[:].rearrange("p (t m) -> p t m", t=PACK), in_=ws[:].rearrange("p (m t) -> p t m", t=PACK)
+        )
+        nc.vector.tensor_copy(xc_raw[:], xs[:].indirect(cand_t[:]))
+        nc.vector.tensor_copy(
+            out=xc_s[:].rearrange("p (t m) -> p t m", t=PACK), in_=xc_raw[:].rearrange("p (m t) -> p t m", t=PACK)
         )
 
         th = []
@@ -136,25 +134,29 @@ def tile_picked_chkmsg_none_po_kernel(
             z_w = keep.tile([P, VH], U32, name="z_w%d" % h, align_bytes=64)
             z_s = keep.tile([P, VH], U8, name="z_s%d" % h, align_bytes=64)
             nc.vector.quantize_mx(out=z_w[:].bitcast(FP8X4), scales=z_s[:], in_=z[:].rearrange("p v t -> p (v t)"))
+            score = psum.tile([P, PACK, VH], F32, name="score%d" % h)
+            for t in range(PACK):
+                rows = slice(P * t, P * (t + 1))
+                nc.tensor.matmul_mx(
+                    out=score[:, t, :], lhsT=xc_w[:, rows].bitcast(FP8X4), lhsT_scale=xc_s[:, rows],
+                    rhs=z_w[:].bitcast(FP8X4), rhs_scale=z_s[:], start=True, stop=True,
+                )
             y = keep.tile([P, PACK, VH], F32, name="y%d" % h, align_bytes=64)
-            for pair in range(2):
-                score = psum.tile([P, 2, VH], F32, name="score%d_%d" % (h, pair))
-                for j in range(2):
-                    rows = slice(P * (2 * pair + j), P * (2 * pair + j + 1))
-                    nc.tensor.matmul_mx(
-                        out=score[:, j, :], lhsT=xc_w[:, rows].bitcast(FP8X4), lhsT_scale=xc_s[:, rows],
-                        rhs=z_w[:].bitcast(FP8X4), rhs_scale=z_s[:], start=True, stop=True,
-                    )
-                nc.scalar.activation(out=y[:, 2 * pair : 2 * pair + 2, :], in_=score[:], func=ACT.Copy, scale=0.0625)
-            nc.sync.dma_start(out=out_rows[:, :, cols], in_=y[:])
             y16 = keep.tile([P, VH, PACK], BF16, name="y16_%d" % h, align_bytes=64)
-            nc.vector.tensor_copy(
-                out=y16[:].rearrange("p (c i) t -> p c t i", i=4), in_=y[:].rearrange("p t (c i) -> p c t i", i=4)
-            )
+            if h == 0:
+                nc.scalar.activation(out=y[:], in_=score[:], func=ACT.Copy, scale=0.0625)
+                nc.vector.tensor_copy(
+                    out=y16[:].rearrange("p (c i) t -> p c t i", i=4), in_=y[:].rearrange("p t (c i) -> p c t i", i=4)
+                )
+                nc.sync.dma_start(out=out_rows[:, :, cols], in_=y[:])
+            else:
+                nc.scalar.activation(out=y16[:], in_=score[:].rearrange("p t v -> p v t"), func=ACT.Copy, scale=0.0625)
+                nc.scalar.activation(out=y[:], in_=score[:], func=ACT.Copy, scale=0.0625)
+                nc.scalar.dma_start(out=out_rows[:, :, cols], in_=y[:])
             nc.vector.quantize_mx(
                 out=o_w[:, cols].bitcast(FP8X4), scales=o_s[:, cols], in_=y16[:].rearrange("p v t -> p (v t)")
             )
             nc.sync.dma_start(out=out_1[0].rearrange("p n t -> p (n t)").bitcast(I32)[:, cols], in_=o_w[:, cols].bitcast(I32))
         for q in range(4):
-            queue = nc.sync if q % 2 else nc.scalar
+            queue = nc.scalar if q == 3 else nc.sync
             queue.dma_start(out=out_2[0, 4 * q : 4 * q + 4, :].bitcast(I32), in_=o_s[32 * q : 32 * q + 4, :].bitcast(I32))

@@ -17,12 +17,16 @@ ALU = mybir.AluOpType
 
 P = 128
 PACK = 4
+QUADRANTS = 4
+STRIPE = 16
+LINE = 4
 HALVES = 2
 VH = V // HALVES
+OUT_SCALE = 0.0625
 
 
 def load_scale_rows(queue, plane, rows):
-    for q in range(4):
+    for q in range(QUADRANTS):
         queue.dma_start(out=plane[32 * q : 32 * q + 4, :].bitcast(I32), in_=rows[4 * q : 4 * q + 4, :].bitcast(I32))
 
 
@@ -34,22 +38,19 @@ def tile_picked_chkmsg_none_po_kernel(
         keep = ctx.enter_context(tc.tile_pool(name="keep", bufs=1))
         psum = ctx.enter_context(tc.psum_pool(name="psum", bufs=1))
 
-        offs_t = keep.tile([P, S // 16], U16, name="offs_t")
-        cand_t = keep.tile([P, C // 16], U16, name="cand_t")
-        c1_t = keep.tile([P, V // 16], U16, name="c1_t")
-        c2_t = keep.tile([P, V // 16], U16, name="c2_t")
+        offs_t = keep.tile([P, S // STRIPE], U16, name="offs_t")
+        cand_t = keep.tile([P, C // STRIPE], U16, name="cand_t")
+        c1_t = keep.tile([P, V // STRIPE], U16, name="c1_t")
+        c2_t = keep.tile([P, V // STRIPE], U16, name="c2_t")
         xs = keep.tile([P, T], U8, name="xs", align_bytes=64)
         ww = keep.tile([P, H], U32, name="ww", align_bytes=64)
         ws = keep.tile([P, H], U8, name="ws", tag="ws", align_bytes=64)
         gain = keep.tile([P, PACK], F32, name="gain")
         offset = keep.tile([P, 1], F32, name="offset")
-        warm = keep.tile([P, 1], F32, name="warm")
-        warm2 = keep.tile([P, 1], F32, name="warm2")
 
         nc.gpsimd.memset(xs[:].bitcast(I32), 0)
         nc.vector.memset(offset[:], 1.125)
         nc.vector.memset(ws[:].bitcast(I32), 0)
-        nc.scalar.activation(out=warm[:], in_=offset[:], func=ACT.Tanh)
         xw = keep.tile([P, T], U32, name="xw", align_bytes=64)
         x_rows = x_words[0].rearrange("p n t -> p (n t)").bitcast(I32)
 
@@ -88,15 +89,14 @@ def tile_picked_chkmsg_none_po_kernel(
         th = []
         for t in range(PACK):
             acc = psum.tile([P, S], F32, name="acc%d" % t)
-            cols = slice(P * t, P * (t + 1))
+            w_cols = slice(P * t, P * (t + 1))
             nc.tensor.matmul_mx(
-                out=acc[:], lhsT=wd_w[:, cols].bitcast(FP8X4), lhsT_scale=wd_s[:, cols],
+                out=acc[:], lhsT=wd_w[:, w_cols].bitcast(FP8X4), lhsT_scale=wd_s[:, w_cols],
                 rhs=xq_w[:].bitcast(FP8X4), rhs_scale=xq_s[:], start=True, stop=True,
             )
             row = keep.tile([P, S], F32, name="th%d" % t, align_bytes=64)
             nc.scalar.activation(out=row[:], in_=acc[:], func=ACT.Tanh, scale=0.5)
             th.append(row)
-        nc.scalar.activation(out=warm2[:], in_=th[PACK - 1][:, 0:1], func=ACT.Ln, bias=offset[:])
 
         xc_w = keep.tile([P, C], U32, name="xc_w", tag="ws", align_bytes=64)
         nc.vector.tensor_copy(xc_w[:].rearrange("p (t m) -> p m t", t=PACK), xw[:].indirect(cand_t[:]))
@@ -104,29 +104,34 @@ def tile_picked_chkmsg_none_po_kernel(
         o_w = keep.tile([P, V], U32, name="o_w", align_bytes=64)
         o_s = keep.tile([P, V], U8, name="o_s", align_bytes=64)
         out_rows = out_0.rearrange("(p t) v -> p t v", t=PACK)
+
         first = keep.tile([P, PACK, V], F32, name="first", align_bytes=64)
         second = keep.tile([P, PACK, VH], F32, name="second", tag="second", align_bytes=64)
         for t in range(PACK):
             nc.vector.tensor_copy(first[:, t, :], th[t][:].indirect(c1_t[:]))
-            nc.vector.tensor_copy(second[:, t, :], th[t][:].indirect(c2_t[:, : VH // 16]))
+            nc.vector.tensor_copy(second[:, t, :], th[t][:].indirect(c2_t[:, : VH // STRIPE]))
         prod_a = keep.tile([P, PACK, VH], F32, name="prod_a", align_bytes=64)
         nc.vector.tensor_tensor(prod_a[:], first[:, :, :VH], second[:], ALU.mult)
         prod_b = keep.tile([P, PACK, VH], F32, name="prod_b", tag="second", align_bytes=64)
         for t in range(PACK):
-            nc.vector.tensor_tensor(prod_b[:, t, :], th[t][:].indirect(c2_t[:, VH // 16 :]), first[:, t, VH:], ALU.mult)
+            nc.vector.tensor_tensor(
+                prod_b[:, t, :], th[t][:].indirect(c2_t[:, VH // STRIPE :]), first[:, t, VH:], ALU.mult
+            )
 
         ups, downs = [], []
         for h, prod in enumerate((prod_a, prod_b)):
             up = keep.tile([P, VH, PACK], F32, name="up%d" % h, align_bytes=64)
             down = keep.tile([P, VH, PACK], F32, name="down%d" % h, align_bytes=64)
-            src = prod[:].rearrange("p t (c i) -> p c t i", i=4)
-            nc.scalar.activation(out=up[:].rearrange("p (c i) t -> p c t i", i=4), in_=src, func=ACT.Ln, bias=offset[:], scale=1.0)
-            nc.scalar.activation(out=down[:].rearrange("p (c i) t -> p c t i", i=4), in_=src, func=ACT.Ln, bias=offset[:], scale=-1.0)
+            src = prod[:].rearrange("p t (c i) -> p c t i", i=LINE)
+            for dst, sign in ((up, 1.0), (down, -1.0)):
+                nc.scalar.activation(
+                    out=dst[:].rearrange("p (c i) t -> p c t i", i=LINE), in_=src, func=ACT.Ln, bias=offset[:], scale=sign
+                )
             ups.append(up)
             downs.append(down)
 
         for h in range(HALVES):
-            cols = slice(h * VH, (h + 1) * VH)
+            checks = slice(h * VH, (h + 1) * VH)
             diff = keep.tile([P, VH, PACK], F32, name="diff%d" % h, align_bytes=64)
             nc.vector.tensor_tensor(diff[:], ups[h][:], downs[h][:], ALU.subtract)
             z = keep.tile([P, VH, PACK], BF16, name="z%d" % h, align_bytes=64)
@@ -134,29 +139,39 @@ def tile_picked_chkmsg_none_po_kernel(
             z_w = keep.tile([P, VH], U32, name="z_w%d" % h, align_bytes=64)
             z_s = keep.tile([P, VH], U8, name="z_s%d" % h, align_bytes=64)
             nc.vector.quantize_mx(out=z_w[:].bitcast(FP8X4), scales=z_s[:], in_=z[:].rearrange("p v t -> p (v t)"))
+
             score = psum.tile([P, PACK, VH], F32, name="score%d" % h)
             for t in range(PACK):
-                rows = slice(P * t, P * (t + 1))
+                cand_cols = slice(P * t, P * (t + 1))
                 nc.tensor.matmul_mx(
-                    out=score[:, t, :], lhsT=xc_w[:, rows].bitcast(FP8X4), lhsT_scale=xc_s[:, rows],
+                    out=score[:, t, :], lhsT=xc_w[:, cand_cols].bitcast(FP8X4), lhsT_scale=xc_s[:, cand_cols],
                     rhs=z_w[:].bitcast(FP8X4), rhs_scale=z_s[:], start=True, stop=True,
                 )
+
             y = keep.tile([P, PACK, VH], F32, name="y%d" % h, align_bytes=64)
             y16 = keep.tile([P, VH, PACK], BF16, name="y16_%d" % h, align_bytes=64)
-            if h == 0:
-                nc.scalar.activation(out=y[:], in_=score[:], func=ACT.Copy, scale=0.0625)
+            if h < HALVES - 1:
+                nc.scalar.activation(out=y[:], in_=score[:], func=ACT.Copy, scale=OUT_SCALE)
                 nc.vector.tensor_copy(
-                    out=y16[:].rearrange("p (c i) t -> p c t i", i=4), in_=y[:].rearrange("p t (c i) -> p c t i", i=4)
+                    out=y16[:].rearrange("p (c i) t -> p c t i", i=LINE),
+                    in_=y[:].rearrange("p t (c i) -> p c t i", i=LINE),
                 )
-                nc.sync.dma_start(out=out_rows[:, :, cols], in_=y[:])
+                nc.sync.dma_start(out=out_rows[:, :, checks], in_=y[:])
             else:
-                nc.scalar.activation(out=y16[:], in_=score[:].rearrange("p t v -> p v t"), func=ACT.Copy, scale=0.0625)
-                nc.scalar.activation(out=y[:], in_=score[:], func=ACT.Copy, scale=0.0625)
-                nc.scalar.dma_start(out=out_rows[:, :, cols], in_=y[:])
+                nc.scalar.activation(
+                    out=y16[:], in_=score[:].rearrange("p t v -> p v t"), func=ACT.Copy, scale=OUT_SCALE
+                )
+                nc.scalar.activation(out=y[:], in_=score[:], func=ACT.Copy, scale=OUT_SCALE)
+                nc.scalar.dma_start(out=out_rows[:, :, checks], in_=y[:])
             nc.vector.quantize_mx(
-                out=o_w[:, cols].bitcast(FP8X4), scales=o_s[:, cols], in_=y16[:].rearrange("p v t -> p (v t)")
+                out=o_w[:, checks].bitcast(FP8X4), scales=o_s[:, checks], in_=y16[:].rearrange("p v t -> p (v t)")
             )
-            nc.sync.dma_start(out=out_1[0].rearrange("p n t -> p (n t)").bitcast(I32)[:, cols], in_=o_w[:, cols].bitcast(I32))
-        for q in range(4):
-            queue = nc.scalar if q == 3 else nc.sync
-            queue.dma_start(out=out_2[0, 4 * q : 4 * q + 4, :].bitcast(I32), in_=o_s[32 * q : 32 * q + 4, :].bitcast(I32))
+            nc.sync.dma_start(
+                out=out_1[0].rearrange("p n t -> p (n t)").bitcast(I32)[:, checks], in_=o_w[:, checks].bitcast(I32)
+            )
+
+        for q in range(QUADRANTS):
+            queue = nc.scalar if q == QUADRANTS - 1 else nc.sync
+            queue.dma_start(
+                out=out_2[0, 4 * q : 4 * q + 4, :].bitcast(I32), in_=o_s[32 * q : 32 * q + 4, :].bitcast(I32)
+            )

from contextlib import ExitStack

import concourse.mybir as mybir

K, T, S, V, H, C = 512, 2048, 512, 256, 512, 512
FLOPS = 2 * K * H * S + 2 * K * C * V

F32 = mybir.dt.float32
BF16 = mybir.dt.bfloat16
I32 = mybir.dt.int32
U32 = mybir.dt.uint32
U16 = mybir.dt.uint16
U8 = mybir.dt.uint8
FP8X4 = mybir.dt.float8_e4m3fn_x4
ACT = mybir.ActivationFunctionType
ALU = mybir.AluOpType

P = 128
PACK = 4
QUADRANTS = 4
STRIPE = 16
LINE = 4
HALVES = 2
VH = V // HALVES
OUT_SCALE = 0.0625


def load_scale_rows(queue, plane, rows):
    for q in range(QUADRANTS):
        queue.dma_start(out=plane[32 * q : 32 * q + 4, :].bitcast(I32), in_=rows[4 * q : 4 * q + 4, :].bitcast(I32))


def tile_picked_chkmsg_none_po_kernel(
    tc, x_words, x_scales, w1_words, w1_scales, gs, offs, c1, c2, cand, out_0, out_1, out_2
):
    nc = tc.nc
    with ExitStack() as ctx:
        keep = ctx.enter_context(tc.tile_pool(name="keep", bufs=1))
        psum = ctx.enter_context(tc.psum_pool(name="psum", bufs=1))

        offs_t = keep.tile([P, S // STRIPE], U16, name="offs_t")
        cand_t = keep.tile([P, C // STRIPE], U16, name="cand_t")
        c1_t = keep.tile([P, V // STRIPE], U16, name="c1_t")
        c2_t = keep.tile([P, V // STRIPE], U16, name="c2_t")
        xs = keep.tile([P, T], U8, name="xs", align_bytes=64)
        ww = keep.tile([P, H], U32, name="ww", align_bytes=64)
        ws = keep.tile([P, H], U8, name="ws", tag="ws", align_bytes=64)
        gain = keep.tile([P, PACK], F32, name="gain")
        offset = keep.tile([P, 1], F32, name="offset")

        nc.gpsimd.memset(xs[:].bitcast(I32), 0)
        nc.vector.memset(offset[:], 1.125)
        nc.vector.memset(ws[:].bitcast(I32), 0)
        xw = keep.tile([P, T], U32, name="xw", align_bytes=64)
        x_rows = x_words[0].rearrange("p n t -> p (n t)").bitcast(I32)

        nc.sync.dma_start(offs_t[:], offs)
        nc.sync.dma_start(out=xw[:, : T // 2].bitcast(I32), in_=x_rows[:, : T // 2])
        load_scale_rows(nc.sync, xs, x_scales[0])
        nc.sync.dma_start(cand_t[:], cand)
        nc.sync.dma_start(out=xw[:, T // 2 :].bitcast(I32), in_=x_rows[:, T // 2 :])
        nc.sync.dma_start(out=ww[:].bitcast(I32), in_=w1_words[0].rearrange("p n t -> p (n t)").bitcast(I32))
        load_scale_rows(nc.sync, ws, w1_scales[0])
        nc.sync.dma_start(c1_t[:], c1)
        nc.sync.dma_start(c2_t[:], c2)
        nc.sync.dma_start(out=gain[:], in_=gs.rearrange("(p t) o -> p (t o)", t=PACK))

        xq_s = keep.tile([P, S], U8, name="xq_s", align_bytes=64)
        xq_w = keep.tile([P, S], U32, name="xq_w", align_bytes=64)
        wd_w = keep.tile([P, H], U32, name="wd_w", align_bytes=64)
        wd_s = keep.tile([P, H], U8, name="wd_s", align_bytes=64)
        xc_raw = keep.tile([P, C], U8, name="xc_raw", align_bytes=64)
        xc_s = keep.tile([P, C], U8, name="xc_s", align_bytes=64)

        nc.vector.tensor_copy(xq_s[:], xs[:].indirect(offs_t[:]))
        nc.vector.tensor_copy(xq_w[:], xw[:].indirect(offs_t[:]))
        nc.vector.tensor_copy(
            out=wd_w[:].bitcast(I32).rearrange("p (t m) -> p m t", t=PACK),
            in_=ww[:].bitcast(I32).rearrange("p (m t) -> p m t", t=PACK),
        )
        nc.vector.tensor_copy(
            out=wd_s[:].rearrange("p (t m) -> p t m", t=PACK), in_=ws[:].rearrange("p (m t) -> p t m", t=PACK)
        )
        nc.vector.tensor_copy(xc_raw[:], xs[:].indirect(cand_t[:]))
        nc.vector.tensor_copy(
            out=xc_s[:].rearrange("p (t m) -> p t m", t=PACK), in_=xc_raw[:].rearrange("p (m t) -> p t m", t=PACK)
        )

        th = []
        for t in range(PACK):
            acc = psum.tile([P, S], F32, name="acc%d" % t)
            w_cols = slice(P * t, P * (t + 1))
            nc.tensor.matmul_mx(
                out=acc[:], lhsT=wd_w[:, w_cols].bitcast(FP8X4), lhsT_scale=wd_s[:, w_cols],
                rhs=xq_w[:].bitcast(FP8X4), rhs_scale=xq_s[:], start=True, stop=True,
            )
            row = keep.tile([P, S], F32, name="th%d" % t, align_bytes=64)
            nc.scalar.activation(out=row[:], in_=acc[:], func=ACT.Tanh, scale=0.5)
            th.append(row)

        xc_w = keep.tile([P, C], U32, name="xc_w", tag="ws", align_bytes=64)
        nc.vector.tensor_copy(xc_w[:].rearrange("p (t m) -> p m t", t=PACK), xw[:].indirect(cand_t[:]))

        o_w = keep.tile([P, V], U32, name="o_w", align_bytes=64)
        o_s = keep.tile([P, V], U8, name="o_s", align_bytes=64)
        out_rows = out_0.rearrange("(p t) v -> p t v", t=PACK)

        first = keep.tile([P, PACK, V], F32, name="first", align_bytes=64)
        second = keep.tile([P, PACK, VH], F32, name="second", tag="second", align_bytes=64)
        for t in range(PACK):
            nc.vector.tensor_copy(first[:, t, :], th[t][:].indirect(c1_t[:]))
            nc.vector.tensor_copy(second[:, t, :], th[t][:].indirect(c2_t[:, : VH // STRIPE]))
        prod_a = keep.tile([P, PACK, VH], F32, name="prod_a", align_bytes=64)
        nc.vector.tensor_tensor(prod_a[:], first[:, :, :VH], second[:], ALU.mult)
        prod_b = keep.tile([P, PACK, VH], F32, name="prod_b", tag="second", align_bytes=64)
        for t in range(PACK):
            nc.vector.tensor_tensor(
                prod_b[:, t, :], th[t][:].indirect(c2_t[:, VH // STRIPE :]), first[:, t, VH:], ALU.mult
            )

        ups, downs = [], []
        for h, prod in enumerate((prod_a, prod_b)):
            up = keep.tile([P, VH, PACK], F32, name="up%d" % h, align_bytes=64)
            down = keep.tile([P, VH, PACK], F32, name="down%d" % h, align_bytes=64)
            src = prod[:].rearrange("p t (c i) -> p c t i", i=LINE)
            for dst, sign in ((up, 1.0), (down, -1.0)):
                nc.scalar.activation(
                    out=dst[:].rearrange("p (c i) t -> p c t i", i=LINE), in_=src, func=ACT.Ln, bias=offset[:], scale=sign
                )
            ups.append(up)
            downs.append(down)

        for h in range(HALVES):
            checks = slice(h * VH, (h + 1) * VH)
            diff = keep.tile([P, VH, PACK], F32, name="diff%d" % h, align_bytes=64)
            nc.vector.tensor_tensor(diff[:], ups[h][:], downs[h][:], ALU.subtract)
            z = keep.tile([P, VH, PACK], BF16, name="z%d" % h, align_bytes=64)
            nc.vector.tensor_tensor(z[:], diff[:], gain[:].unsqueeze(1).to_broadcast([P, VH, PACK]), ALU.mult)
            z_w = keep.tile([P, VH], U32, name="z_w%d" % h, align_bytes=64)
            z_s = keep.tile([P, VH], U8, name="z_s%d" % h, align_bytes=64)
            nc.vector.quantize_mx(out=z_w[:].bitcast(FP8X4), scales=z_s[:], in_=z[:].rearrange("p v t -> p (v t)"))

            score = psum.tile([P, PACK, VH], F32, name="score%d" % h)
            for t in range(PACK):
                cand_cols = slice(P * t, P * (t + 1))
                nc.tensor.matmul_mx(
                    out=score[:, t, :], lhsT=xc_w[:, cand_cols].bitcast(FP8X4), lhsT_scale=xc_s[:, cand_cols],
                    rhs=z_w[:].bitcast(FP8X4), rhs_scale=z_s[:], start=True, stop=True,
                )

            y = keep.tile([P, PACK, VH], F32, name="y%d" % h, align_bytes=64)
            y16 = keep.tile([P, VH, PACK], BF16, name="y16_%d" % h, align_bytes=64)
            if h < HALVES - 1:
                nc.scalar.activation(out=y[:], in_=score[:], func=ACT.Copy, scale=OUT_SCALE)
                nc.vector.tensor_copy(
                    out=y16[:].rearrange("p (c i) t -> p c t i", i=LINE),
                    in_=y[:].rearrange("p t (c i) -> p c t i", i=LINE),
                )
                nc.sync.dma_start(out=out_rows[:, :, checks], in_=y[:])
            else:
                nc.scalar.activation(
                    out=y16[:], in_=score[:].rearrange("p t v -> p v t"), func=ACT.Copy, scale=OUT_SCALE
                )
                nc.scalar.activation(out=y[:], in_=score[:], func=ACT.Copy, scale=OUT_SCALE)
                nc.scalar.dma_start(out=out_rows[:, :, checks], in_=y[:])
            nc.vector.quantize_mx(
                out=o_w[:, checks].bitcast(FP8X4), scales=o_s[:, checks], in_=y16[:].rearrange("p v t -> p (v t)")
            )
            nc.sync.dma_start(
                out=out_1[0].rearrange("p n t -> p (n t)").bitcast(I32)[:, checks], in_=o_w[:, checks].bitcast(I32)
            )

        for q in range(QUADRANTS):
            queue = nc.scalar if q == QUADRANTS - 1 else nc.sync
            queue.dma_start(
                out=out_2[0, 4 * q : 4 * q + 4, :].bitcast(I32), in_=o_s[32 * q : 32 * q + 4, :].bitcast(I32)
            )
